import numpy as np, ml_dtypes
CORES = [3,7,11,15,131,135,139,143]
N = 8
import mx_ref
BF = ml_dtypes.bfloat16
def cols(t, e):
    v = np.concatenate([t.reshape(128, -1, 4), np.zeros((128, 1, 4), BF)], axis=1)
    return np.ascontiguousarray(v[:, e]).reshape(128, -1)
def cut(t, i, w=512):
    return t[:, w * i:w * i + w]
def pick(q, e):
    c = np.concatenate([q[0].reshape(128, -1, 4), np.zeros((128, 1, 4), np.uint8)], axis=1); s = np.concatenate([q[1], np.ones((16, 1), np.uint8)], axis=1)
    return (np.ascontiguousarray(c[:, e].reshape(128, -1)), np.ascontiguousarray(s[:, e]))
def join(*qs):
    return (np.concatenate([q[0] for q in qs], axis=1), np.concatenate([q[1] for q in qs], axis=1))
def put(q, e, v):
    c, s = q[0].reshape(128, -1, 4).copy(), q[1].copy(); c[:, e] = v[0].reshape(128, -1, 4); s[:, e] = v[1]
    return (c.reshape(128, -1), s)
def pk(c, s):
    return (np.ascontiguousarray(c), mx_ref.live(s))
def emit(q):
    return q[0], q[1]
def decode(q):
    o = []
    for b in range(4):
        e = np.zeros((128, 128, 4), np.float32); e[np.arange(128), np.arange(128), b] = 1
        o.append(mx_ref.matmul(mx_ref.quantize(e.reshape(128, 512).astype(BF)), q))
    return np.stack(o, axis=2).reshape(128, -1)
def f(rng, *shape):
    return mx_ref.flush((rng.standard_normal(shape, dtype=np.float32) * np.exp2(rng.integers(-2, 3, shape[:-1] + (1,)))).astype(BF))
def wide(rng, *shape, cols=0):
    v = rng.standard_normal(shape, dtype=np.float32) * np.exp2(rng.integers(-12, 13, shape)).astype(np.float32)
    if cols: v *= np.repeat(np.exp2(rng.integers(-cols, cols + 1, shape[:-2] + (1, shape[-1] // 4))) * (rng.random(shape[:-2] + (1, shape[-1] // 4)) > 0.0625), 4, axis=-1).astype(np.float32)
    return mx_ref.flush(v.astype(BF))
T, C = 128, 32
def best(s):
    return np.argsort(-(s + np.float32(0)), kind="stable")[:C]
def quant(u, v):
    qu = [mx_ref.quantize(np.ascontiguousarray(u[r])) for r in range(N)]
    return qu, [[mx_ref.quantize(np.ascontiguousarray(cut(v[r], i))) for i in range(4)] for r in range(N)]
def layer(q, qu, qv):
    e = best(mx_ref.matmul(qu, q)[0])
    old = pick(q, e)
    a = np.stack([mx_ref.matmul(t, old) for t in qv], axis=2)
    new = np.maximum(a, np.float32(0)) * np.float32(0.05) + decode(old).reshape(128, C, 4)
    return e, new.reshape(128, -1).astype(BF)
def setup_inputs(rng):
    u = np.zeros((N, 128, 512), BF)
    u[:, :, :4] = f(rng, N, 128, 4)
    return {"x": f(rng, N, 128, 4 * T), "u": u, "v": f(rng, N, 128, 2048), "w": f(rng, N, 128, 512)}
def setup_inputs_spread(rng):
    d = setup_inputs(rng)
    d["x"] = wide(rng, N, 128, 4 * T, cols=3)
    return d
def setup_inputs_ties(rng):
    d = setup_inputs(rng)
    d["x"] = np.stack([cols(d["x"][r], rng.permutation(T) % 5 - 1) for r in range(N)])
    d["u"][1::2] = 0
    return d
def setup_inputs_again(rng):
    d = setup_inputs(rng)
    x, u = d["x"].astype(np.float32).reshape(N, 128, T, 4), np.zeros((N, 128, 512), np.float32)
    good = np.stack([rng.permutation(T) < C for r in range(N)])
    x[:, :32] = (1 + rng.random((N, 32, T, 4))) * np.where(good, 1.0, -1.0)[:, None, :, None]
    u[:, :32, :4] = 1 + rng.random((N, 32, 4))
    d["x"], d["u"] = x.reshape(N, 128, 4 * T).astype(BF), u.astype(BF)
    return d
def setup_inputs_other(rng):
    d = setup_inputs(rng)
    x, u = d["x"].astype(np.float32).reshape(N, 128, T, 4), np.zeros((N, 128, 512), np.float32)
    v = d["v"].astype(np.float32).reshape(N, 128, 4, 128, 4)
    large = np.stack([rng.permutation(T) < C for r in range(N)])
    x[:, :16] = (1 + rng.random((N, 16, T, 4))) * np.where(large, 16.0, 1.0)[:, None, :, None]
    x[:, 16:32] = (0.25 + 0.25 * rng.random((N, 16, T, 4))) * rng.choice([-1.0, 1.0], (N, 16, T, 4))
    u[:, :16, :4] = 1 + rng.random((N, 16, 4))
    u[:, 16:32, :4] = -1 - rng.random((N, 16, 4))
    v[:, :, :, 16:32] = 0
    v[:, :16, :, 16:32] = 256 * (1 + rng.random((N, 16, 4, 16, 4)))
    d["x"], d["u"], d["v"] = x.reshape(N, 128, 4 * T).astype(BF), u.astype(BF), v.reshape(N, 128, 2048).astype(BF)
    return d
def setup_inputs_neg(rng):
    d = setup_inputs(rng)
    d["x"] = np.abs(d["x"].astype(np.float32)).astype(BF)
    d["v"] = (-np.abs(d["v"].astype(np.float32))).astype(BF)
    return d
def check_inputs(d):
    b = []
    for k in ("x", "u", "v", "w"):
        a = np.abs(d[k].astype(np.float32))
        if not (np.isfinite(a).all() and ((a == 0) | (a >= 2.0 ** -30) & (a <= 2.0 ** 30)).all()): b.append("a value of " + k)
    if (d["u"][:, :, 4:].astype(np.float32) != 0).any(): b.append("u has numbers behind its column 0")
    if b: return b
    qu, qv = quant(d["u"], d["v"])
    for r in range(N):
        q = mx_ref.quantize(np.ascontiguousarray(d["x"][r]))
        for k in (1, 2):
            e, new = layer(q, qu[(r + k) % N], qv[(r + k) % N])
            a = np.abs(new.astype(np.float32)).reshape(16, 8, C, 4).max(axis=(1, 3))
            if not ((a == 0) | (a >= 2.0 ** -30) & (a <= 2.0 ** 30)).all(): return ["a number of a made column"]
            q = put(q, e, mx_ref.quantize(new))
    return b
def reference(x, u, v, w):
    oc, osc = np.zeros((N, 128, 4 * T), np.uint8), np.zeros((N, 16, T), np.uint8)
    li, y = np.zeros((N, 2, C), np.float32), np.zeros((N, 128, T), np.float32)
    qu, qv = quant(u, v)
    for d in range(N):
        r = (d - 2) % N
        q = mx_ref.quantize(np.ascontiguousarray(x[r]))
        for k in (1, 2):
            s = (r + k) % N
            e, new = layer(q, qu[s], qv[s])
            q = put(q, e, mx_ref.quantize(new))
            li[d, k - 1] = e
        oc[d], osc[d] = emit(q)
        y[d] = mx_ref.matmul(mx_ref.quantize(np.ascontiguousarray(w[d])), q)
    return {"oc": oc, "osc": osc, "li": li, "y": y}

@@ -1,0 +1,262 @@
+from concourse.mybir import dt, AluOpType, ActivationFunctionType
+
+N = 8
+C = 32
+FACTOR = 13421773 * 2.0 ** -28
+FAR = 64.0
+TIE = 2.0 ** -100
+
+SCRATCH = {}
+
+
+def _declare(kind, width, *names):
+    for n in names:
+        SCRATCH[n] = ("sbuf", [128, width], kind)
+
+
+def _pair(width, *names):
+    for n in names:
+        _declare("float8_e4m3fn_x4", width, n)
+        _declare("uint8", width, n + "s")
+
+
+_declare("bfloat16", 512, "xb", "wb", "wo", "wp", "h1", "h2", "n1", "n2")
+_declare("bfloat16", 4, "ub")
+_declare("bfloat16", 1024, "uw")
+_declare("bfloat16", 2048, "vb")
+_declare("bfloat16", 520, "eb")
+_declare("bfloat16", 256, "ob")
+_declare("bfloat16", 128, "tie", "dn", "cb", "f1", "f2", "s1", "s2", "nl1", "nl2", "sl1", "sl2")
+_declare("float32", 128, "ys")
+_declare("float32", 512, "r1", "r2")
+_declare("float32", 1, "pm0", "pnp", "li1", "li2", "lr")
+_declare("float32", 4, "uf")
+_declare("float32", 8, "gs")
+_declare("int32", 1, "pii", "pmi")
+_declare("uint16", 8, "off1", "off2")
+_pair(512, "qv", "qe")
+_pair(256, "win1", "win2")
+_pair(256, "ur")
+_pair(128, "qx", "qw", "qo", "qp", "qh1", "qh2", "t1", "t2")
+for _i in range(8):
+    SCRATCH["p%d" % _i] = ("psum", [128, 512], "float32")
+
+LOADS = ["dx", "du", "dv", "dw"]
+STORES = ["do", "ds0", "ds1", "ds2", "ds3", "dy", "dl1", "dl2"]
+SEMAPHORES = ["cv", "cs", "ct", "cg", "sent", "arr1", "arr2", "arrl"] + LOADS + STORES
+
+
+def rank_program(g, core, T, topo):
+    rank = T.rank_of(core)
+    if rank is None:
+        return
+    A, F = AluOpType, ActivationFunctionType
+    queue = {"v": g.vector, "s": g.scalar, "t": g.tensor, "g": g, "y": g.sync}
+    counter = {"v": "cv", "s": "cs", "t": "ct", "g": "cg"}
+    count = {"v": 0, "s": 0, "t": 0, "g": 0}
+    known = {q: {} for q in queue}
+    wrote, read = {}, {}
+    order = [0]
+
+    def ready(q, reads, writes):
+        need = [wrote[k] for k in list(reads) + list(writes) if k in wrote]
+        for k in writes:
+            need += read.get(k, [])
+        for _, name, val, kn in sorted(need, key=lambda e: -e[0]):
+            if known[q].get(name, 0) < val:
+                queue[q].wait_ge(T.sem[name], val)
+                known[q][name] = val
+            for n2, v2 in kn.items():
+                known[q][n2] = max(known[q].get(n2, 0), v2)
+
+    def done(q, ev, reads, writes):
+        for k in reads:
+            read.setdefault(k, []).append(ev)
+        for k in writes:
+            wrote[k] = ev
+            read[k] = []
+
+    def issue(q, reads, writes, call, *args, **kw):
+        count[q] += 1
+        order[0] += 1
+        call(*args, **kw).then_inc(T.sem[counter[q]], 1)
+        done(q, (order[0], counter[q], count[q], dict(known[q])), reads, writes)
+
+    def op(q, reads, writes, call, *args, **kw):
+        ready(q, reads, writes)
+        issue(q, reads, writes, call, *args, **kw)
+
+    def dma(q, sem, reads, writes, out, in_):
+        ready(q, reads, writes)
+        order[0] += 1
+        queue[q].dma_start(out, in_).then_inc(T.sem[sem], 16)
+        done(q, (order[0], sem, 16, dict(known[q])), reads, writes)
+
+    V, S, E = g.vector, g.scalar, g.tensor
+    nxt, prv = T.cores[(rank + 1) % N], T.cores[(rank - 1) % N]
+
+    def lanes(src, dst, part):
+        es = topo.engines(src, dst)
+        return {"first": es[:8], "last": es[-8:], "all": es}[part]
+
+    sent = [0]
+
+    def send(reads, out, in_, sem, part):
+        ready("g", reads, [])
+        rid, pid = topo.addr(nxt, core)
+        es = lanes(core, nxt, part)
+        sent[0] += len(es)
+        g.remote_dma(out_ap=out, in_ap=in_, remote_sem=T.sem[sem], local_sem=T.sem.sent, pid=pid, routing_id=rid,
+                     dma_engine_mask=sum(1 << e for e in es))
+
+    for key, sem, parts in (("in1", "arr1", ("first", "last")), ("in2", "arr2", ("all", "all")), ("lr", "arrl", ("first",))):
+        wrote[key] = (0, sem, sum(len(lanes(prv, core, p)) for p in parts), {})
+
+    def code(name, a, b):
+        return T[name][:, a:b].bitcast(dt.uint8)
+
+    def quant(key, reads, name, a, in_, n=128):
+        op("v", reads, [key], V.quantize_mx, T[name][:, a:a + n], T[name + "s"][:, a:a + n], in_)
+
+    def act(reads, key, out, in_, func, **kw):
+        op("s", reads, [key], S.activation, out, in_, func, **kw)
+
+    def pick(key, reads, dst, src, off):
+        op("v", reads, [key], V.tensor_copy, T[dst][:, 0:128].bitcast(dt.uint32), T[src][:, 0:256].bitcast(dt.uint32).indirect(off))
+        op("s", reads, [key + "s"], S.activation, T[dst + "s"][:, 0:128], T[src + "s"][:, 0:256].indirect(off), F.Copy)
+
+    dma("y", "dx", [], ["x"], T.xb[:], T.x[:, 0:512])
+    dma("y", "du", [], ["u"], T.ub[:], T.u[:, 0:4])
+    dma("y", "dv", [], ["v"], T.vb[:], T.v[:, 0:2048])
+    dma("y", "dw", ["in1"], ["w"], T.wb[:], T.w[:, 0:512])
+
+    small = dict(allow_small_or_imprecise_dtypes=True)
+    one = T.ob[:, 0:128]
+    wrap = [[0, 8], [-1, 16]]
+
+    def beside(k):
+        for t in (2, 3):
+            op("v", [], ["hz%d%d" % (k, t)], V.memset, T["h%d" % k][:, t:512:4], 0.0)
+
+    def agree(k):
+        op("g", ["ob"], ["hm%d" % k], g.affine_select, T["h%d" % k][:, 1:512:4], one, wrap, A.is_equal, 0.0, 0, 1)
+
+    op("v", [], ["ob"], V.memset, one, 1.0)
+    op("v", [], ["eb"], V.memset, T.eb[:], 0.0)
+    op("v", [], ["om"], V.memset, T.ob[:, 128:256], -1.0)
+    op("g", [], ["pii"], g.iota, T.pii[:], [[0, 1]], 0, 1)
+    op("g", [], ["gs"], g.iota, T.gs[:], [[1, 8]], 64, 0, **small)
+    op("g", ["ob", "eb"], ["e1"], g.affine_select, T.eb[:, 3:515:4], one, [[-1, 128]], A.is_equal, 0.0, 0, 1)
+    beside(1)
+    op("v", ["pii"], ["pmi"], V.tensor_scalar, T.pmi[:], T.pii[:], 15, None, A.bitwise_and)
+    op("v", ["pmi"], ["pm0"], V.tensor_copy, T.pm0[:], T.pmi[:])
+    for t in (0, 2, 3):
+        act(["ob"], "wo%d" % t, T.wo[:, t:512:4], one, F.Copy)
+    act(["ob"], "cb", T.cb[:], one, F.Copy, scale=0.0)
+    act(["gs"], "cb", T.cb[:, 0:128:16], T.gs[:], F.Copy, scale=0.25)
+
+    quant("qx", ["x"], "qx", 0, T.xb[:])
+    send(["qx"], code("win1", 0, 128), code("qx", 0, 128), "arr1", "first")
+    send(["qx"], T.win1s[:, 0:128], T.qxs[:], "arr1", "last")
+    op("g", ["ob"], ["wo1"], g.affine_select, T.wo[:, 1:512:4], one, wrap, A.is_equal, FAR, 0, 1)
+    op("g", ["hz12"], ["tie"], g.affine_select, T.tie[:], T.h1[:, 2:512:4], [[-1, 128]], A.is_ge, TIE, 0, 1)
+    agree(1)
+    op("g", [], ["pnp"], g.iota, T.pnp[:], [[0, 1]], -256, -256, **small)
+    op("g", [], ["dn"], g.iota, T.dn[:], [[-1, 128]], 128, 0, **small)
+
+    act(["u"], "uf", T.uf[:], T.ub[:], F.Copy)
+    for t in range(4):
+        act(["ob", "om", "uf"], "uw%d" % t, T.uw[:, t:1024:4], T.ob[:], F.Identity, scale=T.uf[:, t:t + 1])
+    for b in range(4):
+        quant("qe%d" % b, ["eb", "e1"], "qe", 128 * b, T.eb[:, 3 - b:515 - b])
+    quant("qo", ["wo%d" % t for t in range(4)], "qo", 0, T.wo[:])
+    quant("ur", ["uw%d" % t for t in range(4)], "ur", 0, T.uw[:], 256)
+    for i in range(2):
+        quant("qv%d" % i, ["v"], "qv", 256 * i, T.vb[:, 1024 * i:1024 * i + 1024], 256)
+
+    def mm(reads, bank, w, a, x, b):
+        op("t", reads, [bank], E.matmul_mx, T[bank][:, 0:128], T[w][:, a:a + 128], T[w + "s"][:, a:a + 128],
+           T[x][:, b:b + 128], T[x + "s"][:, b:b + 128], True, True)
+
+    def stop(k):
+        win, key, n, r, qh, h = "win%d" % k, "in%d" % k, "n%d" % k, "r%d" % k, "qh%d" % k, "h%d" % k
+        flag, state, off = "f%d" % k, "s%d" % k, "off%d" % k
+
+        def row(i, bank):
+            mm(["qv%d" % (i // 2), key], bank, "qv", 128 * i, win, 0)
+            act([bank], r + str(i), T[r][:, 128 * i:128 * i + 128], T[bank][:, 0:128], F.Relu, scale=FACTOR)
+
+        def old(i, bank):
+            mm(["qe%d" % i, key], bank, "qe", 128 * i, win, 0)
+
+        def add(i, bank):
+            op("v", [bank, r + str(i)], [n + str(i)], V.tensor_tensor, T[n][:, i:512:4], T[bank][:, 0:128],
+               T[r][:, 128 * i:128 * i + 128], A.add)
+
+        reads = ["ur", key]
+        ready("t", reads, ["p0"])
+        issue("t", reads, ["p0"], E.matmul_mx, T.p0[:, 0:128], T[win][:, 0:128], T[win + "s"][:, 0:128],
+              T.ur[:, 128:256], T.urs[:, 128:256], True, False)
+        issue("t", reads, ["p0"], E.matmul_mx, T.p0[:, 0:128], T.ur[:, 0:128], T.urs[:, 0:128],
+              T[win][:, 0:128], T[win + "s"][:, 0:128], False, True)
+        op("v", ["tie", "p0"], [h], V.tensor_tensor, T[h][:, 0:512:4], T.p0[:, 0:128], T.tie[:], A.is_lt)
+        quant(qh, [h, "hm%d" % k, "hz%d2" % k, "hz%d3" % k], qh, 0, T[h][:])
+        row(0, "p3")
+        old(0, "p4")
+        row(1, "p5")
+        row(2, "p7")
+        old(1, "p6")
+        row(3, "p2")
+        old(2, "p3")
+        mm(["qo", qh], "p1", "qo", 0, qh, 0)
+        act(["p1"], flag, T[flag][:], T.p1[:, 0:128], F.Sign, bias=-0.5 - C)
+        old(3, "p0")
+        add(0, "p4")
+        add(1, "p6")
+        add(2, "p3")
+        add(3, "p0")
+        op("v", ["cb", flag], [state], V.tensor_tensor_scan, T[state][:], T.cb[:], T[flag][:], 0.0, A.max, A.subtract)
+        quant("q" + n, [n + str(i) for i in range(4)], win, 128, T[n][:])
+        op("v", [state, "pm0"], [off], V.tensor_scalar, T[off][:], T[state][:, 15:128:16], 64.0, T.pm0[:, 0:1], A.mult, A.add)
+        if k == 2:
+            ranks(k)
+        pick("t%d" % k, [key, "q" + n, off], "t%d" % k, win, T[off][:])
+
+    def ranks(k):
+        mm(["qp", "qh%d" % k], "p5", "qp", 0, "qh%d" % k, 0)
+        act(["p5", "pnp"], "nl%d" % k, T["nl%d" % k][:], T.p5[:, 0:128], F.Abs, scale=256.0, bias=T.pnp[:, 0:1])
+
+    def places(k):
+        nl, sl, li = "nl%d" % k, "sl%d" % k, "li%d" % k
+        op("v", [nl, "dn"], [sl], V.tensor_tensor_scan, T[sl][:], T[nl][:], T.dn[:], 200.0, A.min, A.max)
+        act([sl], li, T[li][:], T[sl][:, 127:128], F.Copy, scale=-1.0, bias=128.0)
+
+    stop(1)
+    send(["t1"], code("win2", 0, 128), code("t1", 0, 128), "arr2", "all")
+    send(["t1s"], T.win2s[:, 0:128], T.t1s[:], "arr2", "all")
+    agree(2)
+    op("v", [], ["wp"], V.memset, T.wp[:], 1.0)
+    quant("qp", ["wp"], "qp", 0, T.wp[:])
+    beside(2)
+    ranks(1)
+    places(1)
+    send(["li1"], T.lr[:], T.li1[:], "arrl", "first")
+    quant("qw", ["w"], "qw", 0, T.wb[:])
+
+    stop(2)
+
+    dma("y", "dl1", ["lr"], [], T.li[0:1, 0:C], T.lr[0:C, 0:1])
+    dma("y", "do", ["t2"], [], T.oc[:, 0:512], code("t2", 0, 128))
+    mm(["qw", "t2", "t2s"], "p4", "qw", 0, "t2", 0)
+    for k in range(4):
+        dma("yyss"[k], "ds%d" % k, ["t2s"], [], T.osc[4 * k:4 * k + 4, 0:128], T.t2s[32 * k:32 * k + 4, 0:128])
+    places(2)
+    op("v", ["p4"], ["ys"], V.tensor_copy, T.ys[:], T.p4[:, 0:128])
+    dma("s", "dy", ["ys"], [], T.y[:, 0:128], T.ys[:])
+    dma("y", "dl2", ["li2"], [], T.li[1:2, 0:C], T.li2[0:C, 0:1])
+
+    for q in ("v", "s", "t", "g"):
+        g.wait_ge(T.sem[counter[q]], count[q])
+    for s in LOADS + STORES:
+        g.wait_ge(T.sem[s], 16)
+    g.wait_ge(T.sem.sent, sent[0])

@@ -3,7 +3,9 @@ from concourse.mybir import dt, AluOpType, ActivationFunctionType
 N = 8
 C = 32
 FACTOR = 13421773 * 2.0 ** -28
-FAR = 64.0
+STEP = 16.0
+FAR = STEP * C
+LOW = int(FAR - STEP)
 TIE = 2.0 ** -100
 
 SCRATCH = {}
@@ -26,12 +28,11 @@ _declare("bfloat16", 1024, "uw")
 _declare("bfloat16", 2048, "vb")
 _declare("bfloat16", 520, "eb")
 _declare("bfloat16", 256, "ob")
-_declare("bfloat16", 128, "tie", "dn", "cb", "f1", "f2", "s1", "s2", "nl1", "nl2", "sl1", "sl2")
-_declare("float32", 128, "ys")
+_declare("bfloat16", 128, "tie", "dn", "nl1", "nl2", "sl1", "sl2")
+_declare("float32", 128, "ys", "cb", "s1", "s2")
 _declare("float32", 512, "r1", "r2")
 _declare("float32", 1, "pm0", "pnp", "li1", "li2", "lr")
 _declare("float32", 4, "uf")
-_declare("float32", 8, "gs")
 _declare("int32", 1, "pii", "pmi")
 _declare("uint16", 8, "off1", "off2")
 _pair(512, "qv", "qe")
@@ -41,9 +42,9 @@ _pair(128, "qx", "qw", "qo", "qp", "qh1", "qh2", "t1", "t2")
 for _i in range(8):
     SCRATCH["p%d" % _i] = ("psum", [128, 512], "float32")
 
-LOADS = ["dx", "du", "dv", "dw"]
+LOADS = ["dx", "du", "dva", "dvb", "dw"]
 STORES = ["do", "ds0", "ds1", "ds2", "ds3", "dy", "dl1", "dl2"]
-SEMAPHORES = ["cv", "cs", "ct", "cg", "sent", "arr1", "arr2", "arrl"] + LOADS + STORES
+SEMAPHORES = ["cv", "cs", "ct", "cg", "sent", "sent0", "arr1", "arr2", "arrl"] + LOADS + STORES
 
 
 def rank_program(g, core, T, topo):
@@ -94,23 +95,22 @@ def rank_program(g, core, T, topo):
 
     V, S, E = g.vector, g.scalar, g.tensor
     nxt, prv = T.cores[(rank + 1) % N], T.cores[(rank - 1) % N]
+    near = nxt in topo.cores_of(core)
 
-    def lanes(src, dst, part):
-        es = topo.engines(src, dst)
-        return {"first": es[:8], "last": es[-8:], "all": es}[part]
+    sent = {"sent": 0, "sent0": 0}
 
-    sent = [0]
-
-    def send(reads, out, in_, sem, part):
+    def send(reads, out, in_, sem, most=16, local="sent"):
         ready("g", reads, [])
         rid, pid = topo.addr(nxt, core)
-        es = lanes(core, nxt, part)
-        sent[0] += len(es)
-        g.remote_dma(out_ap=out, in_ap=in_, remote_sem=T.sem[sem], local_sem=T.sem.sent, pid=pid, routing_id=rid,
+        es = topo.engines(core, nxt)[:most]
+        sent[local] += len(es)
+        g.remote_dma(out_ap=out, in_ap=in_, remote_sem=T.sem[sem], local_sem=T.sem[local], pid=pid, routing_id=rid,
                      dma_engine_mask=sum(1 << e for e in es))
 
-    for key, sem, parts in (("in1", "arr1", ("first", "last")), ("in2", "arr2", ("all", "all")), ("lr", "arrl", ("first",))):
-        wrote[key] = (0, sem, sum(len(lanes(prv, core, p)) for p in parts), {})
+    lanes = len(topo.engines(prv, core))
+    for key, sem, val in (("in1", "arr1", 2 * lanes), ("in2", "arr2", 2 * lanes), ("lr", "arrl", min(8, lanes)),
+                          ("left", "sent0", len(topo.engines(core, nxt)))):
+        wrote[key] = (0, sem, val, {})
 
     def code(name, a, b):
         return T[name][:, a:b].bitcast(dt.uint8)
@@ -127,7 +127,8 @@ def rank_program(g, core, T, topo):
 
     dma("y", "dx", [], ["x"], T.xb[:], T.x[:, 0:512])
     dma("y", "du", [], ["u"], T.ub[:], T.u[:, 0:4])
-    dma("y", "dv", [], ["v"], T.vb[:], T.v[:, 0:2048])
+    dma("y", "dva", [], ["va"], T.vb[:, 0:1536], T.v[:, 0:1536])
+    dma("y", "dvb", ["left"] if near else [], ["vb"], T.vb[:, 1536:2048], T.v[:, 1536:2048])
     dma("y", "dw", ["in1"], ["w"], T.wb[:], T.w[:, 0:512])
 
     small = dict(allow_small_or_imprecise_dtypes=True)
@@ -141,28 +142,45 @@ def rank_program(g, core, T, topo):
     def agree(k):
         op("g", ["ob"], ["hm%d" % k], g.affine_select, T["h%d" % k][:, 1:512:4], one, wrap, A.is_equal, 0.0, 0, 1)
 
+    def ties():
+        op("g", ["hz13"], ["tie"], g.affine_select, T.tie[:], T.h1[:, 3:512:4], [[-1, 128]], A.is_ge, TIE, 0, 1)
+
+    def later():
+        op("v", [], ["wp0"], V.memset, T.wp[:, 1:512:2], 1.0)
+        op("v", [], ["wp1"], V.memset, T.wp[:, 0:512:4], 1.0)
+        op("v", [], ["wp2"], V.memset, T.wp[:, 2:512:4], 0.0)
+        quant("qp", ["wp0", "wp1", "wp2"], "qp", 0, T.wp[:])
+        beside(2)
+
     op("v", [], ["ob"], V.memset, one, 1.0)
     op("v", [], ["eb"], V.memset, T.eb[:], 0.0)
     op("v", [], ["om"], V.memset, T.ob[:, 128:256], -1.0)
     op("g", [], ["pii"], g.iota, T.pii[:], [[0, 1]], 0, 1)
-    op("g", [], ["gs"], g.iota, T.gs[:], [[1, 8]], 64, 0, **small)
+    agree(1)
     op("g", ["ob", "eb"], ["e1"], g.affine_select, T.eb[:, 3:515:4], one, [[-1, 128]], A.is_equal, 0.0, 0, 1)
     beside(1)
     op("v", ["pii"], ["pmi"], V.tensor_scalar, T.pmi[:], T.pii[:], 15, None, A.bitwise_and)
-    op("v", ["pmi"], ["pm0"], V.tensor_copy, T.pm0[:], T.pmi[:])
-    for t in (0, 2, 3):
-        act(["ob"], "wo%d" % t, T.wo[:, t:512:4], one, F.Copy)
-    act(["ob"], "cb", T.cb[:], one, F.Copy, scale=0.0)
-    act(["gs"], "cb", T.cb[:, 0:128:16], T.gs[:], F.Copy, scale=0.25)
+    op("v", ["pmi"], ["pm0"], V.tensor_scalar, T.pm0[:], T.pmi[:], -16.0 * LOW, None, A.add)
+    act(["ob"], "wo0", T.wo[:, 0:512:4], one, F.Copy, scale=STEP)
+    act(["ob"], "wo2", T.wo[:, 2:512:4], one, F.Copy, scale=0.0)
+    act(["ob"], "wo3", T.wo[:, 3:512:4], one, F.Copy, scale=0.0)
+    act(["hm1"], "wo1", T.wo[:, 1:512:4], T.h1[:, 1:512:4], F.Copy, scale=-FAR, bias=FAR)
+    act(["ob"], "wo0", T.wo[:, 0:512:64], T.ob[:, 0:8], F.Copy, scale=0.0)
+    act(["ob"], "wo2", T.wo[:, 2:512:64], T.ob[:, 0:8], F.Copy, scale=STEP)
+    act(["hm1"], "wo1", T.wo[:, 1:512:64], T.h1[:, 33:512:64], F.Copy, scale=-FAR, bias=FAR)
 
     quant("qx", ["x"], "qx", 0, T.xb[:])
-    send(["qx"], code("win1", 0, 128), code("qx", 0, 128), "arr1", "first")
-    send(["qx"], T.win1s[:, 0:128], T.qxs[:], "arr1", "last")
-    op("g", ["ob"], ["wo1"], g.affine_select, T.wo[:, 1:512:4], one, wrap, A.is_equal, FAR, 0, 1)
-    op("g", ["hz12"], ["tie"], g.affine_select, T.tie[:], T.h1[:, 2:512:4], [[-1, 128]], A.is_ge, TIE, 0, 1)
-    agree(1)
+    if not near:
+        ties()
+    send(["qx"], code("win1", 128, 256), code("qx", 0, 128), "arr1", local="sent0")
+    send(["qx"], T.win1s[:, 128:256], T.qxs[:], "arr1")
+    if near:
+        ties()
+    op("g", [], ["cb"], g.iota, T.cb[:], [[1, 8], [0, 16]], LOW, 0, **small)
+    op("g", [], ["cb"], g.iota, T.cb[:, 0:128:16], [[1, 8]], LOW + 8, 0, **small)
     op("g", [], ["pnp"], g.iota, T.pnp[:], [[0, 1]], -256, -256, **small)
     op("g", [], ["dn"], g.iota, T.dn[:], [[-1, 128]], 128, 0, **small)
+    agree(2)
 
     act(["u"], "uf", T.uf[:], T.ub[:], F.Copy)
     for t in range(4):
@@ -171,8 +189,10 @@ def rank_program(g, core, T, topo):
         quant("qe%d" % b, ["eb", "e1"], "qe", 128 * b, T.eb[:, 3 - b:515 - b])
     quant("qo", ["wo%d" % t for t in range(4)], "qo", 0, T.wo[:])
     quant("ur", ["uw%d" % t for t in range(4)], "ur", 0, T.uw[:], 256)
-    for i in range(2):
-        quant("qv%d" % i, ["v"], "qv", 256 * i, T.vb[:, 1024 * i:1024 * i + 1024], 256)
+    quant("qva", ["va"], "qv", 0, T.vb[:, 0:1536], 384)
+    if near:
+        later()
+    quant("qvb", ["vb"], "qv", 384, T.vb[:, 1536:2048])
 
     def mm(reads, bank, w, a, x, b):
         op("t", reads, [bank], E.matmul_mx, T[bank][:, 0:128], T[w][:, a:a + 128], T[w + "s"][:, a:a + 128],
@@ -180,14 +200,14 @@ def rank_program(g, core, T, topo):
 
     def stop(k):
         win, key, n, r, qh, h = "win%d" % k, "in%d" % k, "n%d" % k, "r%d" % k, "qh%d" % k, "h%d" % k
-        flag, state, off = "f%d" % k, "s%d" % k, "off%d" % k
+        state, off = "s%d" % k, "off%d" % k
 
         def row(i, bank):
-            mm(["qv%d" % (i // 2), key], bank, "qv", 128 * i, win, 0)
+            mm(["qvb" if i == 3 else "qva", key], bank, "qv", 128 * i, win, 128)
             act([bank], r + str(i), T[r][:, 128 * i:128 * i + 128], T[bank][:, 0:128], F.Relu, scale=FACTOR)
 
         def old(i, bank):
-            mm(["qe%d" % i, key], bank, "qe", 128 * i, win, 0)
+            mm(["qe%d" % i, key], bank, "qe", 128 * i, win, 128)
 
         def add(i, bank):
             op("v", [bank, r + str(i)], [n + str(i)], V.tensor_tensor, T[n][:, i:512:4], T[bank][:, 0:128],
@@ -195,11 +215,12 @@ def rank_program(g, core, T, topo):
 
         reads = ["ur", key]
         ready("t", reads, ["p0"])
-        issue("t", reads, ["p0"], E.matmul_mx, T.p0[:, 0:128], T[win][:, 0:128], T[win + "s"][:, 0:128],
+        issue("t", reads, ["p0"], E.matmul_mx, T.p0[:, 0:128], T[win][:, 128:256], T[win + "s"][:, 128:256],
               T.ur[:, 128:256], T.urs[:, 128:256], True, False)
         issue("t", reads, ["p0"], E.matmul_mx, T.p0[:, 0:128], T.ur[:, 0:128], T.urs[:, 0:128],
-              T[win][:, 0:128], T[win + "s"][:, 0:128], False, True)
+              T[win][:, 128:256], T[win + "s"][:, 128:256], False, True)
         op("v", ["tie", "p0"], [h], V.tensor_tensor, T[h][:, 0:512:4], T.p0[:, 0:128], T.tie[:], A.is_lt)
+        op("v", ["tie", "p0"], ["hz%d2" % k], V.tensor_tensor, T[h][:, 34:512:64], T.p0[:, 0:128:16], T.tie[:, 0:128:16], A.is_lt)
         quant(qh, [h, "hm%d" % k, "hz%d2" % k, "hz%d3" % k], qh, 0, T[h][:])
         row(0, "p3")
         old(0, "p4")
@@ -208,16 +229,15 @@ def rank_program(g, core, T, topo):
         old(1, "p6")
         row(3, "p2")
         old(2, "p3")
-        mm(["qo", qh], "p1", "qo", 0, qh, 0)
-        act(["p1"], flag, T[flag][:], T.p1[:, 0:128], F.Sign, bias=-0.5 - C)
         old(3, "p0")
+        mm(["qo", qh], "p1", "qo", 0, qh, 0)
         add(0, "p4")
         add(1, "p6")
         add(2, "p3")
         add(3, "p0")
-        op("v", ["cb", flag], [state], V.tensor_tensor_scan, T[state][:], T.cb[:], T[flag][:], 0.0, A.max, A.subtract)
-        quant("q" + n, [n + str(i) for i in range(4)], win, 128, T[n][:])
-        op("v", [state, "pm0"], [off], V.tensor_scalar, T[off][:], T[state][:, 15:128:16], 64.0, T.pm0[:, 0:1], A.mult, A.add)
+        op("v", ["cb", "p1"], [state], V.tensor_tensor_scan, T[state][:], T.p1[:, 0:128], T.cb[:], 0.0, A.min, A.max)
+        quant("q" + n, [n + str(i) for i in range(4)], win, 0, T[n][:])
+        op("v", [state, "pm0"], [off], V.tensor_scalar, T[off][:], T[state][:, 15:128:16], 16.0, T.pm0[:, 0:1], A.mult, A.add)
         if k == 2:
             ranks(k)
         pick("t%d" % k, [key, "q" + n, off], "t%d" % k, win, T[off][:])
@@ -232,15 +252,13 @@ def rank_program(g, core, T, topo):
         act([sl], li, T[li][:], T[sl][:, 127:128], F.Copy, scale=-1.0, bias=128.0)
 
     stop(1)
-    send(["t1"], code("win2", 0, 128), code("t1", 0, 128), "arr2", "all")
-    send(["t1s"], T.win2s[:, 0:128], T.t1s[:], "arr2", "all")
-    agree(2)
-    op("v", [], ["wp"], V.memset, T.wp[:], 1.0)
-    quant("qp", ["wp"], "qp", 0, T.wp[:])
-    beside(2)
+    send(["t1"], code("win2", 128, 256), code("t1", 0, 128), "arr2")
+    send(["t1s"], T.win2s[:, 128:256], T.t1s[:], "arr2")
+    if not near:
+        later()
     ranks(1)
     places(1)
-    send(["li1"], T.lr[:], T.li1[:], "arrl", "first")
+    send(["li1"], T.lr[:], T.li1[:], "arrl", 8)
     quant("qw", ["w"], "qw", 0, T.wb[:])
 
     stop(2)
@@ -259,4 +277,5 @@ def rank_program(g, core, T, topo):
         g.wait_ge(T.sem[counter[q]], count[q])
     for s in LOADS + STORES:
         g.wait_ge(T.sem[s], 16)
-    g.wait_ge(T.sem.sent, sent[0])
+    for s in sent:
+        g.wait_ge(T.sem[s], sent[s])

from concourse.mybir import dt, AluOpType, ActivationFunctionType

N = 8
C = 32
FACTOR = 13421773 * 2.0 ** -28
STEP = 16.0
FAR = STEP * C
LOW = int(FAR - STEP)
TIE = 2.0 ** -100

SCRATCH = {}


def _declare(kind, width, *names):
    for n in names:
        SCRATCH[n] = ("sbuf", [128, width], kind)


def _pair(width, *names):
    for n in names:
        _declare("float8_e4m3fn_x4", width, n)
        _declare("uint8", width, n + "s")


_declare("bfloat16", 512, "xb", "wb", "wo", "wp", "h1", "h2", "n1", "n2")
_declare("bfloat16", 4, "ub")
_declare("bfloat16", 1024, "uw")
_declare("bfloat16", 2048, "vb")
_declare("bfloat16", 520, "eb")
_declare("bfloat16", 256, "ob")
_declare("bfloat16", 128, "tie", "dn", "nl1", "nl2", "sl1", "sl2")
_declare("float32", 128, "ys", "cb", "s1", "s2")
_declare("float32", 512, "r1", "r2")
_declare("float32", 1, "pm0", "pnp", "li1", "li2", "lr")
_declare("float32", 4, "uf")
_declare("int32", 1, "pii", "pmi")
_declare("uint16", 8, "off1", "off2")
_pair(512, "qv", "qe")
_pair(256, "win1", "win2")
_pair(256, "ur")
_pair(128, "qx", "qw", "qo", "qp", "qh1", "qh2", "t1", "t2")
for _i in range(8):
    SCRATCH["p%d" % _i] = ("psum", [128, 512], "float32")

LOADS = ["dx", "du", "dva", "dvb", "dw"]
STORES = ["do", "ds0", "ds1", "ds2", "ds3", "dy", "dl1", "dl2"]
SEMAPHORES = ["cv", "cs", "ct", "cg", "sent", "sent0", "arr1", "arr2", "arrl"] + LOADS + STORES


def rank_program(g, core, T, topo):
    rank = T.rank_of(core)
    if rank is None:
        return
    A, F = AluOpType, ActivationFunctionType
    queue = {"v": g.vector, "s": g.scalar, "t": g.tensor, "g": g, "y": g.sync}
    counter = {"v": "cv", "s": "cs", "t": "ct", "g": "cg"}
    count = {"v": 0, "s": 0, "t": 0, "g": 0}
    known = {q: {} for q in queue}
    wrote, read = {}, {}
    order = [0]

    def ready(q, reads, writes):
        need = [wrote[k] for k in list(reads) + list(writes) if k in wrote]
        for k in writes:
            need += read.get(k, [])
        for _, name, val, kn in sorted(need, key=lambda e: -e[0]):
            if known[q].get(name, 0) < val:
                queue[q].wait_ge(T.sem[name], val)
                known[q][name] = val
            for n2, v2 in kn.items():
                known[q][n2] = max(known[q].get(n2, 0), v2)

    def done(q, ev, reads, writes):
        for k in reads:
            read.setdefault(k, []).append(ev)
        for k in writes:
            wrote[k] = ev
            read[k] = []

    def issue(q, reads, writes, call, *args, **kw):
        count[q] += 1
        order[0] += 1
        call(*args, **kw).then_inc(T.sem[counter[q]], 1)
        done(q, (order[0], counter[q], count[q], dict(known[q])), reads, writes)

    def op(q, reads, writes, call, *args, **kw):
        ready(q, reads, writes)
        issue(q, reads, writes, call, *args, **kw)

    def dma(q, sem, reads, writes, out, in_):
        ready(q, reads, writes)
        order[0] += 1
        queue[q].dma_start(out, in_).then_inc(T.sem[sem], 16)
        done(q, (order[0], sem, 16, dict(known[q])), reads, writes)

    V, S, E = g.vector, g.scalar, g.tensor
    nxt, prv = T.cores[(rank + 1) % N], T.cores[(rank - 1) % N]
    near = nxt in topo.cores_of(core)

    sent = {"sent": 0, "sent0": 0}

    def send(reads, out, in_, sem, most=16, local="sent"):
        ready("g", reads, [])
        rid, pid = topo.addr(nxt, core)
        es = topo.engines(core, nxt)[:most]
        sent[local] += len(es)
        g.remote_dma(out_ap=out, in_ap=in_, remote_sem=T.sem[sem], local_sem=T.sem[local], pid=pid, routing_id=rid,
                     dma_engine_mask=sum(1 << e for e in es))

    lanes = len(topo.engines(prv, core))
    for key, sem, val in (("in1", "arr1", 2 * lanes), ("in2", "arr2", 2 * lanes), ("lr", "arrl", min(8, lanes)),
                          ("left", "sent0", len(topo.engines(core, nxt)))):
        wrote[key] = (0, sem, val, {})

    def code(name, a, b):
        return T[name][:, a:b].bitcast(dt.uint8)

    def quant(key, reads, name, a, in_, n=128):
        op("v", reads, [key], V.quantize_mx, T[name][:, a:a + n], T[name + "s"][:, a:a + n], in_)

    def act(reads, key, out, in_, func, **kw):
        op("s", reads, [key], S.activation, out, in_, func, **kw)

    def pick(key, reads, dst, src, off):
        op("v", reads, [key], V.tensor_copy, T[dst][:, 0:128].bitcast(dt.uint32), T[src][:, 0:256].bitcast(dt.uint32).indirect(off))
        op("s", reads, [key + "s"], S.activation, T[dst + "s"][:, 0:128], T[src + "s"][:, 0:256].indirect(off), F.Copy)

    dma("y", "dx", [], ["x"], T.xb[:], T.x[:, 0:512])
    dma("y", "du", [], ["u"], T.ub[:], T.u[:, 0:4])
    dma("y", "dva", [], ["va"], T.vb[:, 0:1536], T.v[:, 0:1536])
    dma("y", "dvb", ["left"] if near else [], ["vb"], T.vb[:, 1536:2048], T.v[:, 1536:2048])
    dma("y", "dw", ["in1"], ["w"], T.wb[:], T.w[:, 0:512])

    small = dict(allow_small_or_imprecise_dtypes=True)
    one = T.ob[:, 0:128]
    wrap = [[0, 8], [-1, 16]]

    def beside(k):
        for t in (2, 3):
            op("v", [], ["hz%d%d" % (k, t)], V.memset, T["h%d" % k][:, t:512:4], 0.0)

    def agree(k):
        op("g", ["ob"], ["hm%d" % k], g.affine_select, T["h%d" % k][:, 1:512:4], one, wrap, A.is_equal, 0.0, 0, 1)

    def ties():
        op("g", ["hz13"], ["tie"], g.affine_select, T.tie[:], T.h1[:, 3:512:4], [[-1, 128]], A.is_ge, TIE, 0, 1)

    def later():
        op("v", [], ["wp0"], V.memset, T.wp[:, 1:512:2], 1.0)
        op("v", [], ["wp1"], V.memset, T.wp[:, 0:512:4], 1.0)
        op("v", [], ["wp2"], V.memset, T.wp[:, 2:512:4], 0.0)
        quant("qp", ["wp0", "wp1", "wp2"], "qp", 0, T.wp[:])
        beside(2)

    op("v", [], ["ob"], V.memset, one, 1.0)
    op("v", [], ["eb"], V.memset, T.eb[:], 0.0)
    op("v", [], ["om"], V.memset, T.ob[:, 128:256], -1.0)
    op("g", [], ["pii"], g.iota, T.pii[:], [[0, 1]], 0, 1)
    agree(1)
    op("g", ["ob", "eb"], ["e1"], g.affine_select, T.eb[:, 3:515:4], one, [[-1, 128]], A.is_equal, 0.0, 0, 1)
    beside(1)
    op("v", ["pii"], ["pmi"], V.tensor_scalar, T.pmi[:], T.pii[:], 15, None, A.bitwise_and)
    op("v", ["pmi"], ["pm0"], V.tensor_scalar, T.pm0[:], T.pmi[:], -16.0 * LOW, None, A.add)
    act(["ob"], "wo0", T.wo[:, 0:512:4], one, F.Copy, scale=STEP)
    act(["ob"], "wo2", T.wo[:, 2:512:4], one, F.Copy, scale=0.0)
    act(["ob"], "wo3", T.wo[:, 3:512:4], one, F.Copy, scale=0.0)
    act(["hm1"], "wo1", T.wo[:, 1:512:4], T.h1[:, 1:512:4], F.Copy, scale=-FAR, bias=FAR)
    act(["ob"], "wo0", T.wo[:, 0:512:64], T.ob[:, 0:8], F.Copy, scale=0.0)
    act(["ob"], "wo2", T.wo[:, 2:512:64], T.ob[:, 0:8], F.Copy, scale=STEP)
    act(["hm1"], "wo1", T.wo[:, 1:512:64], T.h1[:, 33:512:64], F.Copy, scale=-FAR, bias=FAR)

    quant("qx", ["x"], "qx", 0, T.xb[:])
    if not near:
        ties()
    send(["qx"], code("win1", 128, 256), code("qx", 0, 128), "arr1", local="sent0")
    send(["qx"], T.win1s[:, 128:256], T.qxs[:], "arr1")
    if near:
        ties()
    op("g", [], ["cb"], g.iota, T.cb[:], [[1, 8], [0, 16]], LOW, 0, **small)
    op("g", [], ["cb"], g.iota, T.cb[:, 0:128:16], [[1, 8]], LOW + 8, 0, **small)
    op("g", [], ["pnp"], g.iota, T.pnp[:], [[0, 1]], -256, -256, **small)
    op("g", [], ["dn"], g.iota, T.dn[:], [[-1, 128]], 128, 0, **small)
    agree(2)

    act(["u"], "uf", T.uf[:], T.ub[:], F.Copy)
    for t in range(4):
        act(["ob", "om", "uf"], "uw%d" % t, T.uw[:, t:1024:4], T.ob[:], F.Identity, scale=T.uf[:, t:t + 1])
    for b in range(4):
        quant("qe%d" % b, ["eb", "e1"], "qe", 128 * b, T.eb[:, 3 - b:515 - b])
    quant("qo", ["wo%d" % t for t in range(4)], "qo", 0, T.wo[:])
    quant("ur", ["uw%d" % t for t in range(4)], "ur", 0, T.uw[:], 256)
    quant("qva", ["va"], "qv", 0, T.vb[:, 0:1536], 384)
    if near:
        later()
    quant("qvb", ["vb"], "qv", 384, T.vb[:, 1536:2048])

    def mm(reads, bank, w, a, x, b):
        op("t", reads, [bank], E.matmul_mx, T[bank][:, 0:128], T[w][:, a:a + 128], T[w + "s"][:, a:a + 128],
           T[x][:, b:b + 128], T[x + "s"][:, b:b + 128], True, True)

    def stop(k):
        win, key, n, r, qh, h = "win%d" % k, "in%d" % k, "n%d" % k, "r%d" % k, "qh%d" % k, "h%d" % k
        state, off = "s%d" % k, "off%d" % k

        def row(i, bank):
            mm(["qvb" if i == 3 else "qva", key], bank, "qv", 128 * i, win, 128)
            act([bank], r + str(i), T[r][:, 128 * i:128 * i + 128], T[bank][:, 0:128], F.Relu, scale=FACTOR)

        def old(i, bank):
            mm(["qe%d" % i, key], bank, "qe", 128 * i, win, 128)

        def add(i, bank):
            op("v", [bank, r + str(i)], [n + str(i)], V.tensor_tensor, T[n][:, i:512:4], T[bank][:, 0:128],
               T[r][:, 128 * i:128 * i + 128], A.add)

        reads = ["ur", key]
        ready("t", reads, ["p0"])
        issue("t", reads, ["p0"], E.matmul_mx, T.p0[:, 0:128], T[win][:, 128:256], T[win + "s"][:, 128:256],
              T.ur[:, 128:256], T.urs[:, 128:256], True, False)
        issue("t", reads, ["p0"], E.matmul_mx, T.p0[:, 0:128], T.ur[:, 0:128], T.urs[:, 0:128],
              T[win][:, 128:256], T[win + "s"][:, 128:256], False, True)
        op("v", ["tie", "p0"], [h], V.tensor_tensor, T[h][:, 0:512:4], T.p0[:, 0:128], T.tie[:], A.is_lt)
        op("v", ["tie", "p0"], ["hz%d2" % k], V.tensor_tensor, T[h][:, 34:512:64], T.p0[:, 0:128:16], T.tie[:, 0:128:16], A.is_lt)
        quant(qh, [h, "hm%d" % k, "hz%d2" % k, "hz%d3" % k], qh, 0, T[h][:])
        row(0, "p3")
        old(0, "p4")
        row(1, "p5")
        row(2, "p7")
        old(1, "p6")
        row(3, "p2")
        old(2, "p3")
        old(3, "p0")
        mm(["qo", qh], "p1", "qo", 0, qh, 0)
        add(0, "p4")
        add(1, "p6")
        add(2, "p3")
        add(3, "p0")
        op("v", ["cb", "p1"], [state], V.tensor_tensor_scan, T[state][:], T.p1[:, 0:128], T.cb[:], 0.0, A.min, A.max)
        quant("q" + n, [n + str(i) for i in range(4)], win, 0, T[n][:])
        op("v", [state, "pm0"], [off], V.tensor_scalar, T[off][:], T[state][:, 15:128:16], 16.0, T.pm0[:, 0:1], A.mult, A.add)
        if k == 2:
            ranks(k)
        pick("t%d" % k, [key, "q" + n, off], "t%d" % k, win, T[off][:])

    def ranks(k):
        mm(["qp", "qh%d" % k], "p5", "qp", 0, "qh%d" % k, 0)
        act(["p5", "pnp"], "nl%d" % k, T["nl%d" % k][:], T.p5[:, 0:128], F.Abs, scale=256.0, bias=T.pnp[:, 0:1])

    def places(k):
        nl, sl, li = "nl%d" % k, "sl%d" % k, "li%d" % k
        op("v", [nl, "dn"], [sl], V.tensor_tensor_scan, T[sl][:], T[nl][:], T.dn[:], 200.0, A.min, A.max)
        act([sl], li, T[li][:], T[sl][:, 127:128], F.Copy, scale=-1.0, bias=128.0)

    stop(1)
    send(["t1"], code("win2", 128, 256), code("t1", 0, 128), "arr2")
    send(["t1s"], T.win2s[:, 128:256], T.t1s[:], "arr2")
    if not near:
        later()
    ranks(1)
    places(1)
    send(["li1"], T.lr[:], T.li1[:], "arrl", 8)
    quant("qw", ["w"], "qw", 0, T.wb[:])

    stop(2)

    dma("y", "dl1", ["lr"], [], T.li[0:1, 0:C], T.lr[0:C, 0:1])
    dma("y", "do", ["t2"], [], T.oc[:, 0:512], code("t2", 0, 128))
    mm(["qw", "t2", "t2s"], "p4", "qw", 0, "t2", 0)
    for k in range(4):
        dma("yyss"[k], "ds%d" % k, ["t2s"], [], T.osc[4 * k:4 * k + 4, 0:128], T.t2s[32 * k:32 * k + 4, 0:128])
    places(2)
    op("v", ["p4"], ["ys"], V.tensor_copy, T.ys[:], T.p4[:, 0:128])
    dma("s", "dy", ["ys"], [], T.y[:, 0:128], T.ys[:])
    dma("y", "dl2", ["li2"], [], T.li[1:2, 0:C], T.li2[0:C, 0:1])

    for q in ("v", "s", "t", "g"):
        g.wait_ge(T.sem[counter[q]], count[q])
    for s in LOADS + STORES:
        g.wait_ge(T.sem[s], 16)
    for s in sent:
        g.wait_ge(T.sem[s], sent[s])
